import numpy as np, ml_dtypes
CORES = [17,81,89,18,82,90]
N = 6
import mx_ref
NC = 128
A = np.float32(0.0125)
BF = ml_dtypes.bfloat16
def cut(t, i, w=512):
    return t[:, w * i:w * i + w]
def tile(rs):
    return np.stack(rs, axis=2).reshape(128, -1).astype(BF)
def pk(c, s, i=0):
    return (np.ascontiguousarray(c[:, 512 * i:512 * i + 512]), mx_ref.live(s[:, 128 * i:128 * i + 128]))
def raw(rng):
    def f(*shape):
        return mx_ref.flush((rng.standard_normal(shape, dtype=np.float32) * np.exp2(rng.integers(-2, 3, shape[:-1] + (1,)))).astype(BF))
    return {"q": f(N, 128, 4 * NC), "k": f(N, 128, 4 * 512), "v": f(N, 128, 512)}
def raw_blocks(rng):
    d = raw(rng)
    for k in ("v",): d[k] = mx_ref.spread(d[k], rng, 4)
    for k in ("q", "k"): d[k] = mx_ref.spread(d[k], rng, 1)
    return d
def raw_wide(rng):
    d = raw(rng)
    for k in ("v",): d[k] = mx_ref.flush((d[k].astype(np.float32) * np.exp2(rng.integers(-8, 9, (N, 1, 1))).astype(np.float32)).astype(BF))
    return d
def raw_sharp(rng):
    d = raw(rng); v = d["q"].astype(np.float32).reshape(N, 128, -1, 4)
    d["q"] = mx_ref.flush((v * np.exp2(rng.integers(-2, 4, (N, 1, v.shape[2], 1))).astype(np.float32)).reshape(d["q"].shape).astype(BF))
    return d
def raw_far(rng):
    d = raw(rng); d["q"] = (d["q"].astype(np.float32) * 10).astype(BF)
    return d
def raw_faroff(rng):
    d = raw(rng); v = d["k"].astype(np.float32).reshape(N, 128, -1, 4)
    d["k"] = mx_ref.flush((v + 192 * rng.standard_normal((1, 128, 1, 4), dtype=np.float32)).reshape(d["k"].shape).astype(BF))
    return d
def pack(d, rng):
    o = {"q": d["q"]}
    for m in ("k", "v"):
        t = d[m]; c = np.zeros(t.shape, np.uint8); s = np.zeros((N, 128, t.shape[2] // 4), np.uint8)
        for r in range(N):
            for i in range(t.shape[2] // 512):
                a, b = mx_ref.quantize(cut(t[r], i)); c[r][:, 512 * i:512 * i + 512] = a; s[r][:, 128 * i:128 * i + 128] = mx_ref.plane(b, rng)
        o[m + "c"], o[m + "s"] = c, s
    return o
def setup_inputs(rng):
    return pack(raw(rng), rng)
def setup_inputs_blocks(rng):
    return pack(raw_blocks(rng), rng)
def setup_inputs_far(rng):
    return pack(raw_far(rng), rng)
def setup_inputs_faroff(rng):
    return pack(raw_faroff(rng), rng)
def setup_inputs_sharp(rng):
    return pack(raw_sharp(rng), rng)
def setup_inputs_wide(rng):
    return pack(raw_wide(rng), rng)
def reference(q, kc, ks, vc, vs, own=None):
    ONE = mx_ref.quantize(np.ones((128, 512), BF))
    K = [[pk(kc[j], ks[j], b) for b in range(4)] for j in range(N)]; V = [pk(vc[j], vs[j]) for j in range(N)]
    Q = [mx_ref.quantize(q[i]) for i in range(N)]
    lo = np.zeros((N, N, NC), np.float32); w = lo.copy(); wlo = lo.copy(); whi = lo.copy(); p = np.zeros((N, N, 128, 4 * NC), BF); o = np.zeros((N, 128, NC), np.float32)
    S = [[[mx_ref.matmul(K[j][b], Q[i]) * A for b in range(4)] for i in range(N)] for j in range(N)]
    for j in range(N):
        lo[j] = [np.max(s, axis=(0, 1)) for s in S[j]]
    hi = np.broadcast_to(lo.max(axis=0) + 8, lo.shape).copy()
    c = lo if own is None else own["c"]
    for j in range(N):
        for i in range(N):
            p[j][i] = tile([np.exp(np.maximum(s - c[j][i], -20).astype(np.float64)).astype(np.float32) for s in S[j][i]])
    use = p if own is None else own["p"]
    for i in range(N):
        e = np.exp((c[:, i] - c[:, i].max(axis=0)).astype(np.float64)); wlo[i] = e * (1 - 4e-5); whi[i] = e * (1 + 4e-5)
        w[i] = e if own is None else own["w"][i]
        num = den = 0
        for j in range(N):
            P = mx_ref.quantize(use[j][i])
            num = num + w[i][j].astype(np.float64) * mx_ref.matmul(V[j], P); den = den + w[i][j].astype(np.float64) * mx_ref.matmul(ONE, P)
        o[i] = (num / den).astype(np.float32)
    return {"c": c, "c__lo": lo, "c__hi": hi, "p": p, "w": w, "w__lo": wlo, "w__hi": whi, "o": o}

@@ -1,0 +1,365 @@
+import math
+from concourse.bass import DstId, RemoteDMATransfer
+from concourse.mybir import dt, AluOpType, AxisListType, ActivationFunctionType as AF
+
+N = 6
+SIM = 96
+W = 132
+F = 0.0125
+
+ORDER = [[0, 3, 5, 1, 2, 4], [1, 4, 5, 0, 2, 3], [2, 5, 3, 4, 0, 1], [3, 0, 1, 4, 5, 2], [4, 1, 0, 3, 5, 2], [5, 2, 3, 4, 0, 1]]
+QORD = [[3, 4, 1], [4, 3, 0], [5], [0, 2, 5, 4, 1], [1, 2, 5, 3, 0], [2, 0, 1, 3, 4]]
+LATE = [[5, 2], [5, 2], [0, 1], [1, 2], [0, 2], [0, 1]]
+
+SCRATCH = {
+    "qt": ("sbuf", [128, 512], "bfloat16"),
+    "onet": ("sbuf", [128, 512], "bfloat16"),
+    "kcd": ("sbuf", [128, 512], "float8_e4m3fn_x4"),
+    "ksc": ("sbuf", [128, 512], "uint8"),
+    "vo": ("sbuf", [128, 256], "float8_e4m3fn_x4"),
+    "vos": ("sbuf", [128, 256], "uint8"),
+    "pc": ("sbuf", [128, 128 * N], "float8_e4m3fn_x4"),
+    "pp": ("sbuf", [128, 128 * N], "uint8"),
+    "x": ("sbuf", [128, 512 * N], "bfloat16"),
+    "yt": ("sbuf", [128, 512 * N], "bfloat16"),
+    "sb": ("sbuf", [128, W * N], "float32"),
+    "land": ("sbuf", [128, 7 * W], "float32"),
+    "u": ("sbuf", [128, 7 * 128], "float32"),
+    "m20": ("sbuf", [128, 1], "float32"),
+    "e20": ("sbuf", [128, 1], "float32"),
+    "nm": ("sbuf", [128, 8], "float32"),
+    "nb": ("sbuf", [128, 8], "float32"),
+    "cc": ("sbuf", [128, 32], "float32"),
+    "ct": ("sbuf", [128, 32], "float32"),
+    "cw": ("sbuf", [128, 32], "float32"),
+    "wt": ("sbuf", [128, 32], "float32"),
+    "we": ("sbuf", [128, 4], "float32"),
+    "pe": ("sbuf", [128, 4], "float32"),
+    "ex": ("sbuf", [128, 4], "float32"),
+    "pl": ("sbuf", [128, 4], "float32"),
+    "sm": ("sbuf", [128, 8], "float32"),
+    "v1": ("sbuf", [128, 128], "float32"),
+    "v2": ("sbuf", [128, 128], "float32"),
+    "t1": ("sbuf", [128, 128], "float32"),
+    "t2": ("sbuf", [128, 128], "float32"),
+    "t3": ("sbuf", [128, 128], "float32"),
+    "ot": ("sbuf", [128, 128], "float32"),
+    "ps": ("psum", [128, 512 * N], "float32"),
+}
+for _i in range(N):
+    SCRATCH["qc%d" % _i] = ("sbuf", [128, 128], "float8_e4m3fn_x4")
+    SCRATCH["qs%d" % _i] = ("sbuf", [128, 128], "uint8")
+    SCRATCH["p%d" % _i] = ("sbuf", [128, 512], "bfloat16")
+
+SEMAPHORES = ["lq", "lk", "lv", "loc", "ms", "m2", "e2", "oq", "qq", "st", "st2", "zc", "cn", "cx"]
+for _i in range(N):
+    SEMAPHORES += ["%s%d" % (_n, _i) for _n in ("qa", "qb", "aa", "ps", "mx", "nb", "xa", "xb", "tr", "cp", "pq", "pa", "ev")]
+SEMAPHORES += ["h%d" % _i for _i in range(22)]
+
+
+def bits(m):
+    return bin(m).count("1")
+
+
+def plan(T, topo):
+    relay = []
+    for s in range(N):
+        src = T.cores[s]
+        far = [d for d in range(N) if d != s and not topo.may_write(src, T.cores[d])]
+        far.sort(key=lambda d: (topo.chip(T.cores[d]), d))
+        r = {}
+        if far:
+            hs = [h for h in range(SIM) if topo.chip(h) == topo.chip(src) and h not in T.cores
+                  and topo.may_write(src, h) and all(topo.may_write(h, T.cores[d]) for d in far)]
+            hs.sort(key=lambda h: (topo.die(h) == topo.die(src), h))
+            half = (len(far) + 1) // 2
+            for k, d in enumerate(far):
+                r[d] = hs[0 if k < half else 1]
+        relay.append(r)
+    return relay
+
+
+def transfer(T, topo, core, dsts, mask, sem, buf):
+    ids = []
+    for d in dsts:
+        a = topo.addr(d)
+        ids.append(DstId(rid=a[0], pnc=a[1]))
+    return RemoteDMATransfer(dst_ids=ids, dma_engine_mask=mask, remote_sem=T.sem[sem], srcs=[buf], dsts=[buf for d in dsts])
+
+
+def slot(home, src):
+    late = LATE[home]
+    early = [j for j in range(N) if j not in late]
+    return (early + late).index(src)
+
+
+def q_parts(T, topo, relay, s):
+    src = T.cores[s]
+    dst = []
+    for h in relay[s].values():
+        if h not in dst:
+            dst.append(h)
+    dst += [T.cores[d] for d in QORD[s]]
+    on = [c for c in dst if topo.chip(c) == topo.chip(src)]
+    off = [c for c in dst if topo.chip(c) != topo.chip(src)]
+    parts = []
+    if off:
+        m = topo.mask(src, off[0])
+        parts.append((off, m))
+        parts.append((on, topo.mask(src, on[0]) & ~m))
+    else:
+        parts.append((on, topo.mask(src, on[0])))
+    return parts
+
+
+def q_count(T, topo, relay, s, dst):
+    for cores, m in q_parts(T, topo, relay, s):
+        if dst in cores:
+            return bits(m)
+    h = relay[s][T.rank_of(dst)]
+    return bits(topo.mask(h, dst))
+
+
+def send_row(g, T, topo, core, dst, out, src, sem):
+    a = topo.addr(dst)
+    m = topo.mask(core, dst)
+    g.remote_dma(out_ap=out, in_ap=src, remote_sem=T.sem[sem], local_sem=T.sem["loc"], pid=a[1], routing_id=a[0], dma_engine_mask=m)
+    return bits(m)
+
+
+def helper_program(g, core, T, topo, relay):
+    for s in range(N):
+        mine = [d for d in relay[s] if relay[s][d] == core]
+        if not mine:
+            continue
+        n = q_count(T, topo, relay, s, core)
+        dst = [T.cores[d] for d in mine]
+        m = topo.mask(core, dst[0])
+        g.wait_ge(T.sem["qa%d" % s], n)
+        g.remote_dma_fused([transfer(T, topo, core, dst, m, "qa%d" % s, T["qc%d" % s][:].bitcast(dt.uint8))], local_sem=T.sem["loc"])
+        g.wait_ge(T.sem["qb%d" % s], n)
+        g.remote_dma_fused([transfer(T, topo, core, dst, m, "qb%d" % s, T["qs%d" % s][:])], local_sem=T.sem["loc"])
+        loc = 2 * bits(m)
+        for i in ORDER[s]:
+            if i in mine:
+                g.wait_ge(T.sem["aa%d" % i], bits(topo.mask(T.cores[s], core)))
+                k = W * slot(i, s)
+                loc += send_row(g, T, topo, core, T.cores[i], T.land[:, k:k + 130], T.sb[:, W * i:W * i + 130], "aa%d" % s)
+        g.wait_ge(T.sem["loc"], loc)
+
+
+def rank_program(g, core, T, topo):
+    rank = T.rank_of(core)
+    relay = plan(T, topo)
+    if rank is None:
+        helper_program(g, core, T, topo, relay)
+        return
+    S = T.sem
+    v, a, t, y = g.vector, g.scalar, g.tensor, g.sync
+    order = ORDER[rank]
+    late = LATE[rank]
+    early = [j for j in range(N) if j not in late]
+    own = slot(rank, rank)
+
+    def bank(i, lo, hi):
+        return T.ps[:, 512 * i + lo:512 * i + hi]
+
+    def rowbuf(i, lo, hi):
+        if i == rank:
+            return T.land[:, W * own + lo:W * own + hi]
+        return T.sb[:, W * i + lo:W * i + hi]
+
+    def part(buf, i, lo=0, hi=128):
+        return T[buf][:, 128 * i + lo:128 * i + hi]
+
+    y.dma_start(T.qt[:], T.q[:]).then_inc(S.lq, 16)
+    y.dma_start(T.kcd[:].bitcast(dt.uint8), T.kc[:]).then_inc(S.lk, 16)
+    y.dma_start(T.ksc[:], T.ks[:]).then_inc(S.lk, 16)
+    y.dma_start(T.vo[:, 0:128].bitcast(dt.uint8), T.vc[:]).then_inc(S.lv, 16)
+    y.dma_start(T.vos[:, 0:128], T.vs[:]).then_inc(S.lv, 16)
+
+    v.memset(T.m20[:], -20.0).then_inc(S.m2, 1)
+    v.memset(T.onet[:], 1.0).then_inc(S.ms, 1)
+    v.memset(T.cc[:], 0.0).then_inc(S.zc, 1)
+    v.memset(T.cw[:], 0.0).then_inc(S.zc, 1)
+    v.wait_ge(S.ms, 1)
+    v.quantize_mx(T.vo[:, 128:256], T.vos[:, 128:256], T.onet[:]).then_inc(S.oq, 1)
+    v.wait_ge(S.lq, 16)
+    v.quantize_mx(T["qc%d" % rank][:], T["qs%d" % rank][:], T.qt[:]).then_inc(S.qq, 1)
+    a.wait_ge(S.m2, 1)
+    a.activation(T.e20[:], T.m20[:], AF.Exp).then_inc(S.e2, 1)
+
+    loc = 0
+    parts = q_parts(T, topo, relay, rank)
+    g.wait_ge(S.qq, 1)
+    for sem, buf in (("qa%d" % rank, T["qc%d" % rank][:].bitcast(dt.uint8)), ("qb%d" % rank, T["qs%d" % rank][:])):
+        g.remote_dma_fused([transfer(T, topo, core, d, m, sem, buf) for d, m in parts], local_sem=S.loc)
+        loc += sum(bits(m) for d, m in parts)
+
+    def scores(i):
+        if i == rank:
+            t.wait_ge(S.qq, 1)
+            t.wait_ge(S.lk, 32)
+        else:
+            n = q_count(T, topo, relay, i, core)
+            t.wait_ge(S["qa%d" % i], n)
+            t.wait_ge(S["qb%d" % i], n)
+        t.matmul_mx(bank(i, 0, 512), T["qc%d" % i][:], T["qs%d" % i][:], T.kcd[:], T.ksc[:], True, True).then_inc(S["ps%d" % i], 1)
+
+    scores(order[0])
+    t.wait_ge(S.lv, 32)
+    t.wait_ge(S.oq, 1)
+    for k in range(N):
+        if k + 1 < N:
+            scores(order[k + 1])
+        i = order[k]
+        t.wait_ge(S["pq%d" % i], 1)
+        t.matmul_mx(bank(i, 0, 256), part("pc", i), part("pp", i), T.vo[:, 0:256], T.vos[:, 0:256], True, True).then_inc(S["pa%d" % i], 1)
+
+    def shift(i):
+        v.wait_ge(S["ps%d" % i], 1)
+        v.tensor_reduce(T.nm[:, i:i + 1], bank(i, 0, 512), AxisListType.X, AluOpType.max, negate=True).then_inc(S["mx%d" % i], 1)
+        v.wait_ge(S["mx%d" % i], 1)
+        v.tensor_scalar(T.nb[:, i:i + 1], T.nm[:, i:i + 1], F, None, AluOpType.mult).then_inc(S["nb%d" % i], 1)
+
+    shift(order[0])
+    v.wait_ge(S.e2, 1)
+    for k in range(N):
+        i = order[k]
+        p = T["p%d" % i]
+        o = 512 * i
+        for b in range(4):
+            if b == 0:
+                v.wait_ge(S["xa%d" % i], 1)
+            if b == 2:
+                v.wait_ge(S["xb%d" % i], 1)
+            v.transpose(T.yt[:, o + b:o + 512:4], T.x[:, o + 128 * b:o + 128 * b + 128]).then_inc(S["tr%d" % i], 1)
+        if k + 1 < N:
+            shift(order[k + 1])
+        v.wait_ge(S["tr%d" % i], 4)
+        for d in range(4):
+            for q in range(4):
+                v.tensor_scalar(p[32 * d:32 * d + 32, 128 * q:128 * q + 128], T.yt[32 * q:32 * q + 32, o + 128 * d:o + 128 * d + 128],
+                                T.e20[32 * q:32 * q + 32, 0:1], None, AluOpType.max).then_inc(S["cp%d" % i], 1)
+        v.wait_ge(S["cp%d" % i], 16)
+        v.quantize_mx(part("pc", i), part("pp", i), p[:]).then_inc(S["pq%d" % i], 1)
+
+    def exps(i):
+        o = 512 * i
+        a.wait_ge(S["nb%d" % i], 1)
+        a.activation(T.x[:, o:o + 256], bank(i, 0, 256), AF.Exp, bias=T.nb[:, i:i + 1], scale=F).then_inc(S["xa%d" % i], 1)
+        a.activation(T.x[:, o + 256:o + 512], bank(i, 256, 512), AF.Exp, bias=T.nb[:, i:i + 1], scale=F).then_inc(S["xb%d" % i], 1)
+        a.activation(rowbuf(i, 129, 130), T.nb[:, i:i + 1], AF.Copy, scale=-1.0).then_inc(S["ev%d" % i], 1)
+
+    exps(order[0])
+    for k in range(N):
+        if k + 1 < N:
+            exps(order[k + 1])
+        i = order[k]
+        a.wait_ge(S["pa%d" % i], 1)
+        a.activation(rowbuf(i, 0, 129), bank(i, 0, 129), AF.Copy).then_inc(S["ev%d" % i], 1)
+
+    for i in order:
+        if i == rank:
+            continue
+        g.wait_ge(S["ev%d" % i], 2)
+        k = W * slot(i, rank)
+        if i in relay[rank]:
+            loc += send_row(g, T, topo, core, relay[rank][i], rowbuf(i, 0, 130), rowbuf(i, 0, 130), "aa%d" % i)
+        else:
+            loc += send_row(g, T, topo, core, T.cores[i], T.land[:, k:k + 130], rowbuf(i, 0, 130), "aa%d" % rank)
+
+    v.wait_ge(S.zc, 2)
+    v.wait_ge(S["nb%d" % order[-1]], 1)
+    v.tensor_scalar(T.cc[:, 0:N], T.nb[:, 0:N], -1.0, None, AluOpType.mult).then_inc(S.cn, 1)
+    v.wait_ge(S.cn, 1)
+    v.transpose(T.ct[:], T.cc[:]).then_inc(S.cx, 1)
+    for i in order:
+        y.wait_ge(S["cp%d" % i], 16)
+        y.dma_start(T.p[i], T["p%d" % i][:]).then_inc(S.st, 16)
+    y.wait_ge(S.cx, 1)
+    for q in range(4):
+        y.dma_start(T.c[:, 32 * q:32 * q + 32], T.ct[32 * q:32 * q + N, 0:32]).then_inc(S.st, 16)
+
+    def arrived(queue, j):
+        if j == rank:
+            queue.wait_ge(S["ev%d" % rank], 2)
+        else:
+            h = relay[j].get(rank, T.cores[j])
+            queue.wait_ge(S["aa%d" % j], bits(topo.mask(h, core)))
+
+    def cols(first, n, c):
+        lo = W * first + c
+        return T.land[:, lo:lo + (n - 1) * W + 1:W]
+
+    E = 6 * W
+    for j in early:
+        arrived(v, j)
+    v.tensor_reduce(T.sm[:, 0:1], cols(0, 4, 129), AxisListType.X, AluOpType.max, negate=True).then_inc(S.h0, 1)
+    v.wait_ge(S.h0, 1)
+    v.tensor_scalar(T.land[:, E + 129:E + 130], T.sm[:, 0:1], -1.0, None, AluOpType.mult).then_inc(S.h1, 1)
+    a.wait_ge(S.h0, 1)
+    a.activation(T.we[:, 0:4], cols(0, 4, 129), AF.Exp, bias=T.sm[:, 0:1]).then_inc(S.h2, 1)
+    a.wait_ge(S.h2, 1)
+    for k in range(4):
+        a.activation(part("u", k), T.land[:, W * k:W * k + 128], AF.Copy, scale=T.we[:, k:k + 1]).then_inc(S.h3 if k < 2 else S.h4, 1)
+    v.wait_ge(S.h2, 1)
+    v.tensor_tensor(T.pe[:, 0:4], T.we[:, 0:4], cols(0, 4, 128), AluOpType.mult).then_inc(S.h5, 1)
+    v.wait_ge(S.h5, 1)
+    v.tensor_reduce(T.land[:, E + 128:E + 129], T.pe[:, 0:4], AxisListType.X, AluOpType.add).then_inc(S.h6, 1)
+    v.wait_ge(S.h3, 2)
+    v.tensor_tensor(T.v1[:], part("u", 0), part("u", 1), AluOpType.add).then_inc(S.h7, 1)
+    v.wait_ge(S.h4, 2)
+    v.tensor_tensor(T.v2[:], part("u", 2), part("u", 3), AluOpType.add).then_inc(S.h7, 1)
+    v.wait_ge(S.h7, 2)
+    v.tensor_tensor(T.land[:, E:E + 128], T.v1[:], T.v2[:], AluOpType.add).then_inc(S.h8, 1)
+
+    v.wait_ge(S.h1, 1)
+    for j in late:
+        arrived(v, j)
+    v.tensor_reduce(T.sm[:, 1:2], cols(4, 3, 129), AxisListType.X, AluOpType.max, negate=True).then_inc(S.h9, 1)
+    a.wait_ge(S.h9, 1)
+    a.activation(T.ex[:, 0:3], cols(4, 3, 129), AF.Exp, bias=T.sm[:, 1:2]).then_inc(S.h10, 1)
+    a.wait_ge(S.h10, 1)
+    a.wait_ge(S.h8, 1)
+    for k in (4, 5, 6):
+        a.activation(part("u", k), T.land[:, W * k:W * k + 128], AF.Copy, scale=T.ex[:, k - 4:k - 3]).then_inc(S.h11 if k < 6 else S.h12, 1)
+    v.wait_ge(S.h6, 1)
+    v.wait_ge(S.h10, 1)
+    v.tensor_tensor(T.pl[:, 0:3], T.ex[:, 0:3], cols(4, 3, 128), AluOpType.mult).then_inc(S.h13, 1)
+    v.wait_ge(S.h13, 1)
+    v.tensor_reduce(T.sm[:, 2:3], T.pl[:, 0:3], AxisListType.X, AluOpType.add).then_inc(S.h14, 1)
+    v.wait_ge(S.h14, 1)
+    v.reciprocal(T.sm[:, 3:4], T.sm[:, 2:3]).then_inc(S.h15, 1)
+    v.wait_ge(S.h11, 2)
+    v.tensor_tensor(T.t1[:], part("u", 4), part("u", 5), AluOpType.add).then_inc(S.h16, 1)
+    v.wait_ge(S.h16, 1)
+    v.wait_ge(S.h12, 1)
+    v.tensor_tensor(T.t2[:], T.t1[:], part("u", 6), AluOpType.add).then_inc(S.h17, 1)
+    v.wait_ge(S.h17, 1)
+    v.wait_ge(S.h15, 1)
+    v.tensor_scalar(T.t3[:], T.t2[:], T.sm[:, 3:4], None, AluOpType.mult).then_inc(S.h18, 1)
+    v.wait_ge(S.h18, 1)
+    for b in range(4):
+        v.transpose(T.ot[:, 32 * b:32 * b + 32], T.t3[:, b:128:4]).then_inc(S.h19, 1)
+    a.wait_ge(S.zc, 2)
+    for k, j in enumerate(early):
+        a.activation(T.cw[:, j:j + 1], T.we[:, k:k + 1], AF.Copy, scale=T.ex[:, 2:3]).then_inc(S.h20, 1)
+    for k, j in enumerate(late):
+        a.activation(T.cw[:, j:j + 1], T.ex[:, k:k + 1], AF.Copy).then_inc(S.h20, 1)
+    v.wait_ge(S.h20, N)
+    v.transpose(T.wt[:], T.cw[:]).then_inc(S.h21, 1)
+
+    y.wait_ge(S.h19, 4)
+    a.wait_ge(S.h19, 4)
+    for q in range(4):
+        queue, sem = (y, S.st) if q < 2 else (a, S.st2)
+        queue.dma_start(T.o[:, 32 * q:32 * q + 32], T.ot[32 * q:32 * q + 32, :]).then_inc(sem, 16)
+    y.wait_ge(S.h21, 1)
+    a.wait_ge(S.h21, 1)
+    for q in range(4):
+        queue, sem = (y, S.st) if q < 2 else (a, S.st2)
+        queue.dma_start(T.w[:, 32 * q:32 * q + 32], T.wt[32 * q:32 * q + N, 0:32]).then_inc(sem, 16)
+    y.wait_ge(S.st, 16 * (N + 4 + 4))
+    a.wait_ge(S.st2, 16 * 4)
+    g.wait_ge(S.loc, loc)

@@ -6,10 +6,12 @@ N = 6
 SIM = 96
 W = 132
 F = 0.0125
+NS = 1
+GG = 2
 
-ORDER = [[0, 3, 5, 1, 2, 4], [1, 4, 5, 0, 2, 3], [2, 5, 3, 4, 0, 1], [3, 0, 1, 4, 5, 2], [4, 1, 0, 3, 5, 2], [5, 2, 3, 4, 0, 1]]
-QORD = [[3, 4, 1], [4, 3, 0], [5], [0, 2, 5, 4, 1], [1, 2, 5, 3, 0], [2, 0, 1, 3, 4]]
-LATE = [[5, 2], [5, 2], [0, 1], [1, 2], [0, 2], [0, 1]]
+ORDER = [[0, 3, 1, 5, 2, 4], [1, 3, 0, 2, 5, 4], [2, 4, 3, 1, 0, 5], [3, 1, 0, 4, 2, 5], [4, 0, 1, 5, 3, 2], [5, 4, 2, 3, 1, 0]]
+QORD = [[3, 4, 1], [3, 4, 0], [5], [2, 1, 0, 5, 4], [2, 5, 3, 1, 0], [0, 1, 4, 3, 2]]
+LATE = [[5, 2], [4, 0], [4, 0], [1, 2], [0, 1], [3, 1]]
 
 SCRATCH = {
     "qt": ("sbuf", [128, 512], "bfloat16"),
@@ -20,6 +22,8 @@ SCRATCH = {
     "vos": ("sbuf", [128, 256], "uint8"),
     "pc": ("sbuf", [128, 128 * N], "float8_e4m3fn_x4"),
     "pp": ("sbuf", [128, 128 * N], "uint8"),
+    "hs": ("sbuf", [128, 256 * N], "float32"),
+    "mx": ("sbuf", [128, 256 * N], "float32"),
     "x": ("sbuf", [128, 512 * N], "bfloat16"),
     "yt": ("sbuf", [128, 512 * N], "bfloat16"),
     "sb": ("sbuf", [128, W * N], "float32"),
@@ -27,7 +31,6 @@ SCRATCH = {
     "u": ("sbuf", [128, 7 * 128], "float32"),
     "m20": ("sbuf", [128, 1], "float32"),
     "e20": ("sbuf", [128, 1], "float32"),
-    "nm": ("sbuf", [128, 8], "float32"),
     "nb": ("sbuf", [128, 8], "float32"),
     "cc": ("sbuf", [128, 32], "float32"),
     "ct": ("sbuf", [128, 32], "float32"),
@@ -53,7 +56,7 @@ for _i in range(N):
 
 SEMAPHORES = ["lq", "lk", "lv", "loc", "ms", "m2", "e2", "oq", "qq", "st", "st2", "zc", "cn", "cx"]
 for _i in range(N):
-    SEMAPHORES += ["%s%d" % (_n, _i) for _n in ("qa", "qb", "aa", "ps", "mx", "nb", "xa", "xb", "tr", "cp", "pq", "pa", "ev")]
+    SEMAPHORES += ["%s%d" % (_n, _i) for _n in ("qa", "qb", "aa", "ps", "mx", "nb", "xa", "xb", "hc", "sc", "tr", "cp", "pq", "pa", "ev")]
 SEMAPHORES += ["h%d" % _i for _i in range(22)]
 
 
@@ -192,9 +195,11 @@ def rank_program(g, core, T, topo):
     loc = 0
     parts = q_parts(T, topo, relay, rank)
     g.wait_ge(S.qq, 1)
-    for sem, buf in (("qa%d" % rank, T["qc%d" % rank][:].bitcast(dt.uint8)), ("qb%d" % rank, T["qs%d" % rank][:])):
-        g.remote_dma_fused([transfer(T, topo, core, d, m, sem, buf) for d, m in parts], local_sem=S.loc)
-        loc += sum(bits(m) for d, m in parts)
+    for lo in range(0, max(len(d) for d, m in parts), GG):
+        now = [(d[lo:lo + GG], m) for d, m in parts if d[lo:lo + GG]]
+        for sem, buf in (("qa%d" % rank, T["qc%d" % rank][:].bitcast(dt.uint8)), ("qb%d" % rank, T["qs%d" % rank][:])):
+            g.remote_dma_fused([transfer(T, topo, core, d, m, sem, buf) for d, m in now], local_sem=S.loc)
+            loc += sum(bits(m) for d, m in now)
 
     def scores(i):
         if i == rank:
@@ -207,20 +212,22 @@ def rank_program(g, core, T, topo):
         t.matmul_mx(bank(i, 0, 512), T["qc%d" % i][:], T["qs%d" % i][:], T.kcd[:], T.ksc[:], True, True).then_inc(S["ps%d" % i], 1)
 
     scores(order[0])
+    scores(order[1])
     t.wait_ge(S.lv, 32)
     t.wait_ge(S.oq, 1)
     for k in range(N):
-        if k + 1 < N:
-            scores(order[k + 1])
+        if k + 2 < N:
+            scores(order[k + 2])
         i = order[k]
         t.wait_ge(S["pq%d" % i], 1)
         t.matmul_mx(bank(i, 0, 256), part("pc", i), part("pp", i), T.vo[:, 0:256], T.vos[:, 0:256], True, True).then_inc(S["pa%d" % i], 1)
 
     def shift(i):
-        v.wait_ge(S["ps%d" % i], 1)
-        v.tensor_reduce(T.nm[:, i:i + 1], bank(i, 0, 512), AxisListType.X, AluOpType.max, negate=True).then_inc(S["mx%d" % i], 1)
+        m = 256 * i
+        v.wait_ge(S["hc%d" % i], 1)
+        v.tensor_tensor_scan(T.mx[:, m:m + 256], bank(i, 0, 256), T.hs[:, m:m + 256], -1e29, AluOpType.max, AluOpType.max).then_inc(S["mx%d" % i], 1)
         v.wait_ge(S["mx%d" % i], 1)
-        v.tensor_scalar(T.nb[:, i:i + 1], T.nm[:, i:i + 1], F, None, AluOpType.mult).then_inc(S["nb%d" % i], 1)
+        v.tensor_scalar(T.nb[:, i:i + 1], T.mx[:, m + 255:m + 256], -F, None, AluOpType.mult).then_inc(S["nb%d" % i], 1)
 
     shift(order[0])
     v.wait_ge(S.e2, 1)
@@ -237,12 +244,19 @@ def rank_program(g, core, T, topo):
         if k + 1 < N:
             shift(order[k + 1])
         v.wait_ge(S["tr%d" % i], 4)
-        for d in range(4):
-            for q in range(4):
+        for q in range(NS, 4):
+            for d in range(4):
                 v.tensor_scalar(p[32 * d:32 * d + 32, 128 * q:128 * q + 128], T.yt[32 * q:32 * q + 32, o + 128 * d:o + 128 * d + 128],
                                 T.e20[32 * q:32 * q + 32, 0:1], None, AluOpType.max).then_inc(S["cp%d" % i], 1)
+        if NS:
+            v.wait_ge(S["sc%d" % i], 4 * NS)
+            v.tensor_scalar(p[:, 0:128 * NS], p[:, 0:128 * NS], T.e20[:, 0:1], None, AluOpType.max).then_inc(S["cp%d" % i], 4 * NS)
         v.wait_ge(S["cp%d" % i], 16)
         v.quantize_mx(part("pc", i), part("pp", i), p[:]).then_inc(S["pq%d" % i], 1)
+
+    def half(i):
+        a.wait_ge(S["ps%d" % i], 1)
+        a.activation(T.hs[:, 256 * i:256 * i + 256], bank(i, 256, 512), AF.Copy).then_inc(S["hc%d" % i], 1)
 
     def exps(i):
         o = 512 * i
@@ -251,11 +265,21 @@ def rank_program(g, core, T, topo):
         a.activation(T.x[:, o + 256:o + 512], bank(i, 256, 512), AF.Exp, bias=T.nb[:, i:i + 1], scale=F).then_inc(S["xb%d" % i], 1)
         a.activation(rowbuf(i, 129, 130), T.nb[:, i:i + 1], AF.Copy, scale=-1.0).then_inc(S["ev%d" % i], 1)
 
+    half(order[0])
     exps(order[0])
+    half(order[1])
     for k in range(N):
+        i = order[k]
+        if NS:
+            a.wait_ge(S["tr%d" % i], 4)
+        for q in range(NS):
+            for d in range(4):
+                o = 512 * i + 128 * d
+                a.activation(T["p%d" % i][32 * d:32 * d + 32, 128 * q:128 * q + 128], T.yt[32 * q:32 * q + 32, o:o + 128], AF.Copy).then_inc(S["sc%d" % i], 1)
         if k + 1 < N:
             exps(order[k + 1])
-        i = order[k]
+        if k + 2 < N:
+            half(order[k + 2])
         a.wait_ge(S["pa%d" % i], 1)
         a.activation(rowbuf(i, 0, 129), bank(i, 0, 129), AF.Copy).then_inc(S["ev%d" % i], 1)
 
@@ -315,48 +339,50 @@ def rank_program(g, core, T, topo):
     v.tensor_tensor(T.land[:, E:E + 128], T.v1[:], T.v2[:], AluOpType.add).then_inc(S.h8, 1)
 
     v.wait_ge(S.h1, 1)
+    v.wait_ge(S.h6, 1)
+    v.wait_ge(S.h8, 1)
     for j in late:
         arrived(v, j)
     v.tensor_reduce(T.sm[:, 1:2], cols(4, 3, 129), AxisListType.X, AluOpType.max, negate=True).then_inc(S.h9, 1)
     a.wait_ge(S.h9, 1)
     a.activation(T.ex[:, 0:3], cols(4, 3, 129), AF.Exp, bias=T.sm[:, 1:2]).then_inc(S.h10, 1)
     a.wait_ge(S.h10, 1)
-    a.wait_ge(S.h8, 1)
-    for k in (4, 5, 6):
-        a.activation(part("u", k), T.land[:, W * k:W * k + 128], AF.Copy, scale=T.ex[:, k - 4:k - 3]).then_inc(S.h11 if k < 6 else S.h12, 1)
-    v.wait_ge(S.h6, 1)
+    for k in (4, 5):
+        a.activation(part("u", k), T.land[:, W * k:W * k + 128], AF.Copy, scale=T.ex[:, k - 4:k - 3]).then_inc(S["h%d" % (k + 7)], 1)
     v.wait_ge(S.h10, 1)
     v.tensor_tensor(T.pl[:, 0:3], T.ex[:, 0:3], cols(4, 3, 128), AluOpType.mult).then_inc(S.h13, 1)
+    v.tensor_scalar(part("u", 6), T.land[:, E:E + 128], T.ex[:, 2:3], None, AluOpType.mult).then_inc(S.h16, 1)
     v.wait_ge(S.h13, 1)
     v.tensor_reduce(T.sm[:, 2:3], T.pl[:, 0:3], AxisListType.X, AluOpType.add).then_inc(S.h14, 1)
+    v.wait_ge(S.h11, 1)
+    v.wait_ge(S.h16, 1)
+    v.tensor_tensor(T.t1[:], part("u", 4), part("u", 6), AluOpType.add).then_inc(S.h17, 1)
     v.wait_ge(S.h14, 1)
     v.reciprocal(T.sm[:, 3:4], T.sm[:, 2:3]).then_inc(S.h15, 1)
-    v.wait_ge(S.h11, 2)
-    v.tensor_tensor(T.t1[:], part("u", 4), part("u", 5), AluOpType.add).then_inc(S.h16, 1)
-    v.wait_ge(S.h16, 1)
-    v.wait_ge(S.h12, 1)
-    v.tensor_tensor(T.t2[:], T.t1[:], part("u", 6), AluOpType.add).then_inc(S.h17, 1)
     v.wait_ge(S.h17, 1)
-    v.wait_ge(S.h15, 1)
-    v.tensor_scalar(T.t3[:], T.t2[:], T.sm[:, 3:4], None, AluOpType.mult).then_inc(S.h18, 1)
+    v.wait_ge(S.h12, 1)
+    v.tensor_tensor(T.t2[:], T.t1[:], part("u", 5), AluOpType.add).then_inc(S.h18, 1)
     v.wait_ge(S.h18, 1)
-    for b in range(4):
-        v.transpose(T.ot[:, 32 * b:32 * b + 32], T.t3[:, b:128:4]).then_inc(S.h19, 1)
+    v.wait_ge(S.h15, 1)
+    v.tensor_scalar(T.t3[:], T.t2[:], T.sm[:, 3:4], None, AluOpType.mult).then_inc(S.h20, 1)
     a.wait_ge(S.zc, 2)
     for k, j in enumerate(early):
-        a.activation(T.cw[:, j:j + 1], T.we[:, k:k + 1], AF.Copy, scale=T.ex[:, 2:3]).then_inc(S.h20, 1)
+        a.activation(T.cw[:, j:j + 1], T.we[:, k:k + 1], AF.Copy, scale=T.ex[:, 2:3]).then_inc(S.h21, 1)
     for k, j in enumerate(late):
-        a.activation(T.cw[:, j:j + 1], T.ex[:, k:k + 1], AF.Copy).then_inc(S.h20, 1)
-    v.wait_ge(S.h20, N)
-    v.transpose(T.wt[:], T.cw[:]).then_inc(S.h21, 1)
+        a.activation(T.cw[:, j:j + 1], T.ex[:, k:k + 1], AF.Copy).then_inc(S.h21, 1)
+    v.wait_ge(S.h20, 1)
+    for b in range(4):
+        v.transpose(T.ot[:, 32 * b:32 * b + 32], T.t3[:, b:128:4]).then_inc(S.h19, 1)
+    v.wait_ge(S.h21, N)
+    v.transpose(T.wt[:], T.cw[:]).then_inc(S.cn, 1)
 
     y.wait_ge(S.h19, 4)
     a.wait_ge(S.h19, 4)
     for q in range(4):
         queue, sem = (y, S.st) if q < 2 else (a, S.st2)
         queue.dma_start(T.o[:, 32 * q:32 * q + 32], T.ot[32 * q:32 * q + 32, :]).then_inc(sem, 16)
-    y.wait_ge(S.h21, 1)
-    a.wait_ge(S.h21, 1)
+    y.wait_ge(S.cn, 2)
+    a.wait_ge(S.cn, 2)
     for q in range(4):
         queue, sem = (y, S.st) if q < 2 else (a, S.st2)
         queue.dma_start(T.w[:, 32 * q:32 * q + 32], T.wt[32 * q:32 * q + N, 0:32]).then_inc(sem, 16)

@@ -6,12 +6,15 @@ N = 6
 SIM = 96
 W = 132
 F = 0.0125
-NS = 1
-GG = 2
+GG = 1
 
-ORDER = [[0, 3, 1, 5, 2, 4], [1, 3, 0, 2, 5, 4], [2, 4, 3, 1, 0, 5], [3, 1, 0, 4, 2, 5], [4, 0, 1, 5, 3, 2], [5, 4, 2, 3, 1, 0]]
-QORD = [[3, 4, 1], [3, 4, 0], [5], [2, 1, 0, 5, 4], [2, 5, 3, 1, 0], [0, 1, 4, 3, 2]]
-LATE = [[5, 2], [4, 0], [4, 0], [1, 2], [0, 1], [3, 1]]
+ORDER = [[0, 3, 5, 1, 2, 4], [1, 4, 0, 5, 2, 3], [2, 4, 3, 1, 0, 5], [3, 1, 0, 2, 5, 4], [4, 0, 1, 3, 5, 2], [5, 3, 4, 2, 0, 1]]
+QORD = [[4, 3, 1], [3, 4, 0], [5], [5, 0, 2, 4, 1], [2, 5, 1, 0, 3], [0, 4, 1, 2, 3]]
+LATE = [[1, 2], [5, 0], [1, 4, 0], [5, 1], [3, 0], [2, 3]]
+MOVE = ["aaaavvvvvvvvvvvv"] * 6
+VT = ("R0 V0 C0 Q0 M1 N1 R1 M2 V1:0:2 N2 V1:2:16 C1 R2 Q1 M3 V2:0:2 N3 V2:2:16 C2 R3 Q2 M4 V3:0:2 N4 V3:2:16 C3 R4 Q3 "
+      "M5 V4:0:2 N5 V4:2:16 C4 R5 Q4 V5 C5 Q5")
+AT = "X0 A0 H1 X1 H2 A1 E0 X2 H3 A2 E1 X3 H4 A3 E2 X4 H5 A4 E3 X5 A5 E4 E5"
 
 SCRATCH = {
     "qt": ("sbuf", [128, 512], "bfloat16"),
@@ -26,25 +29,26 @@ SCRATCH = {
     "mx": ("sbuf", [128, 256 * N], "float32"),
     "x": ("sbuf", [128, 512 * N], "bfloat16"),
     "yt": ("sbuf", [128, 512 * N], "bfloat16"),
+    "z": ("sbuf", [128, 512 * N], "bfloat16"),
     "sb": ("sbuf", [128, W * N], "float32"),
     "land": ("sbuf", [128, 7 * W], "float32"),
-    "u": ("sbuf", [128, 7 * 128], "float32"),
+    "ue": ("sbuf", [128, 512], "float32"),
+    "ul": ("sbuf", [128, 512], "float32"),
+    "fe": ("sbuf", [128, 512], "float32"),
+    "fl": ("sbuf", [128, 512], "float32"),
+    "se": ("sbuf", [128, 512], "float32"),
+    "sl": ("sbuf", [128, 512], "float32"),
     "m20": ("sbuf", [128, 1], "float32"),
     "e20": ("sbuf", [128, 1], "float32"),
-    "nb": ("sbuf", [128, 8], "float32"),
     "cc": ("sbuf", [128, 32], "float32"),
     "ct": ("sbuf", [128, 32], "float32"),
     "cw": ("sbuf", [128, 32], "float32"),
     "wt": ("sbuf", [128, 32], "float32"),
     "we": ("sbuf", [128, 4], "float32"),
-    "pe": ("sbuf", [128, 4], "float32"),
     "ex": ("sbuf", [128, 4], "float32"),
+    "pe": ("sbuf", [128, 4], "float32"),
     "pl": ("sbuf", [128, 4], "float32"),
     "sm": ("sbuf", [128, 8], "float32"),
-    "v1": ("sbuf", [128, 128], "float32"),
-    "v2": ("sbuf", [128, 128], "float32"),
-    "t1": ("sbuf", [128, 128], "float32"),
-    "t2": ("sbuf", [128, 128], "float32"),
     "t3": ("sbuf", [128, 128], "float32"),
     "ot": ("sbuf", [128, 128], "float32"),
     "ps": ("psum", [128, 512 * N], "float32"),
@@ -54,10 +58,10 @@ for _i in range(N):
     SCRATCH["qs%d" % _i] = ("sbuf", [128, 128], "uint8")
     SCRATCH["p%d" % _i] = ("sbuf", [128, 512], "bfloat16")
 
-SEMAPHORES = ["lq", "lk", "lv", "loc", "ms", "m2", "e2", "oq", "qq", "st", "st2", "zc", "cn", "cx"]
+SEMAPHORES = ["lq", "lk", "lv", "loc", "ms", "m2", "e2", "oq", "qq", "st", "st2", "zc", "cn", "cx", "oc", "wx", "f1", "f2"]
 for _i in range(N):
-    SEMAPHORES += ["%s%d" % (_n, _i) for _n in ("qa", "qb", "aa", "ps", "mx", "nb", "xa", "xb", "hc", "sc", "tr", "cp", "pq", "pa", "ev")]
-SEMAPHORES += ["h%d" % _i for _i in range(22)]
+    SEMAPHORES += ["%s%d" % (_n, _i) for _n in ("qa", "qb", "aa", "ps", "mx", "nb", "xa", "xb", "hc", "zm", "tr", "cp", "pq", "pa", "ev")]
+SEMAPHORES += ["h%d" % _i for _i in range(17)]
 
 
 def bits(m):
@@ -93,7 +97,7 @@ def transfer(T, topo, core, dsts, mask, sem, buf):
 def slot(home, src):
     late = LATE[home]
     early = [j for j in range(N) if j not in late]
-    return (early + late).index(src)
+    return len(early) + 1 + late.index(src) if src in late else early.index(src)
 
 
 def q_parts(T, topo, relay, s):
@@ -151,6 +155,17 @@ def helper_program(g, core, T, topo, relay):
         g.wait_ge(T.sem["loc"], loc)
 
 
+def blocks(k, who):
+    return [(n // 4, n % 4) for n in range(16) if MOVE[k][n] == who]
+
+
+def groups(k):
+    n = 0
+    while n < 4 and MOVE[k][4 * n:4 * n + 4] != "vvvv":
+        n += 1
+    return n
+
+
 def rank_program(g, core, T, topo):
     rank = T.rank_of(core)
     relay = plan(T, topo)
@@ -162,18 +177,22 @@ def rank_program(g, core, T, topo):
     order = ORDER[rank]
     late = LATE[rank]
     early = [j for j in range(N) if j not in late]
-    own = slot(rank, rank)
+    ne, nl = len(early), 1 + len(late)
 
     def bank(i, lo, hi):
         return T.ps[:, 512 * i + lo:512 * i + hi]
 
     def rowbuf(i, lo, hi):
         if i == rank:
-            return T.land[:, W * own + lo:W * own + hi]
+            k = W * slot(rank, rank)
+            return T.land[:, k + lo:k + hi]
         return T.sb[:, W * i + lo:W * i + hi]
 
-    def part(buf, i, lo=0, hi=128):
-        return T[buf][:, 128 * i + lo:128 * i + hi]
+    def shift(i):
+        return T.sb[:, W * i + 129:W * i + 130]
+
+    def part(buf, i):
+        return T[buf][:, 128 * i:128 * i + 128]
 
     y.dma_start(T.qt[:], T.q[:]).then_inc(S.lq, 16)
     y.dma_start(T.kcd[:].bitcast(dt.uint8), T.kc[:]).then_inc(S.lk, 16)
@@ -189,6 +208,10 @@ def rank_program(g, core, T, topo):
     v.quantize_mx(T.vo[:, 128:256], T.vos[:, 128:256], T.onet[:]).then_inc(S.oq, 1)
     v.wait_ge(S.lq, 16)
     v.quantize_mx(T["qc%d" % rank][:], T["qs%d" % rank][:], T.qt[:]).then_inc(S.qq, 1)
+    for buf, sem, n in (("fe", S.f1, ne), ("fl", S.f2, nl)):
+        v.memset(T[buf][:, 0:n * 128], 1.0).then_inc(sem, 1)
+        v.wait_ge(sem, 1)
+        v.memset(T[buf][:, 0:n * 128:n], 0.0).then_inc(sem, 1)
     a.wait_ge(S.m2, 1)
     a.activation(T.e20[:], T.m20[:], AF.Exp).then_inc(S.e2, 1)
 
@@ -222,71 +245,82 @@ def rank_program(g, core, T, topo):
         t.wait_ge(S["pq%d" % i], 1)
         t.matmul_mx(bank(i, 0, 256), part("pc", i), part("pp", i), T.vo[:, 0:256], T.vos[:, 0:256], True, True).then_inc(S["pa%d" % i], 1)
 
-    def shift(i):
-        m = 256 * i
-        v.wait_ge(S["hc%d" % i], 1)
-        v.tensor_tensor_scan(T.mx[:, m:m + 256], bank(i, 0, 256), T.hs[:, m:m + 256], -1e29, AluOpType.max, AluOpType.max).then_inc(S["mx%d" % i], 1)
-        v.wait_ge(S["mx%d" % i], 1)
-        v.tensor_scalar(T.nb[:, i:i + 1], T.mx[:, m + 255:m + 256], -F, None, AluOpType.mult).then_inc(S["nb%d" % i], 1)
-
-    shift(order[0])
-    v.wait_ge(S.e2, 1)
-    for k in range(N):
+    def place(k, q, d):
         i = order[k]
-        p = T["p%d" % i]
-        o = 512 * i
-        for b in range(4):
-            if b == 0:
-                v.wait_ge(S["xa%d" % i], 1)
-            if b == 2:
-                v.wait_ge(S["xb%d" % i], 1)
-            v.transpose(T.yt[:, o + b:o + 512:4], T.x[:, o + 128 * b:o + 128 * b + 128]).then_inc(S["tr%d" % i], 1)
-        if k + 1 < N:
-            shift(order[k + 1])
-        v.wait_ge(S["tr%d" % i], 4)
-        for q in range(NS, 4):
-            for d in range(4):
-                v.tensor_scalar(p[32 * d:32 * d + 32, 128 * q:128 * q + 128], T.yt[32 * q:32 * q + 32, o + 128 * d:o + 128 * d + 128],
-                                T.e20[32 * q:32 * q + 32, 0:1], None, AluOpType.max).then_inc(S["cp%d" % i], 1)
-        if NS:
-            v.wait_ge(S["sc%d" % i], 4 * NS)
-            v.tensor_scalar(p[:, 0:128 * NS], p[:, 0:128 * NS], T.e20[:, 0:1], None, AluOpType.max).then_inc(S["cp%d" % i], 4 * NS)
-        v.wait_ge(S["cp%d" % i], 16)
-        v.quantize_mx(part("pc", i), part("pp", i), p[:]).then_inc(S["pq%d" % i], 1)
+        if q < groups(k):
+            return T.z[32 * d:32 * d + 32, 512 * i + 128 * q:512 * i + 128 * q + 128]
+        return T["p%d" % i][32 * d:32 * d + 32, 128 * q:128 * q + 128]
 
-    def half(i):
-        a.wait_ge(S["ps%d" % i], 1)
-        a.activation(T.hs[:, 256 * i:256 * i + 256], bank(i, 256, 512), AF.Copy).then_inc(S["hc%d" % i], 1)
+    def made(k):
+        gz = groups(k)
+        direct = len([1 for q, d in blocks(k, "v") if q >= gz])
+        return 4 * gz, direct + (1 if gz else 0)
 
-    def exps(i):
-        o = 512 * i
-        a.wait_ge(S["nb%d" % i], 1)
-        a.activation(T.x[:, o:o + 256], bank(i, 0, 256), AF.Exp, bias=T.nb[:, i:i + 1], scale=F).then_inc(S["xa%d" % i], 1)
-        a.activation(T.x[:, o + 256:o + 512], bank(i, 256, 512), AF.Exp, bias=T.nb[:, i:i + 1], scale=F).then_inc(S["xb%d" % i], 1)
-        a.activation(rowbuf(i, 129, 130), T.nb[:, i:i + 1], AF.Copy, scale=-1.0).then_inc(S["ev%d" % i], 1)
-
-    half(order[0])
-    exps(order[0])
-    half(order[1])
-    for k in range(N):
+    def vector(s, k, lo, hi):
         i = order[k]
-        if NS:
+        o, m = 512 * i, 256 * i
+        if s == "M":
+            v.wait_ge(S["hc%d" % i], 1)
+            v.tensor_tensor_scan(T.mx[:, m:m + 256], bank(i, 0, 256), T.hs[:, m:m + 256], -1e29, AluOpType.max, AluOpType.max).then_inc(S["mx%d" % i], 1)
+        elif s == "N":
+            v.wait_ge(S["mx%d" % i], 1)
+            v.tensor_scalar(shift(i), T.mx[:, m + 255:m + 256], -F, None, AluOpType.mult).then_inc(S["nb%d" % i], 1)
+        elif s == "R":
+            for b in range(4):
+                if b == 0:
+                    v.wait_ge(S["xa%d" % i], 1)
+                if b == 2:
+                    v.wait_ge(S["xb%d" % i], 1)
+                v.transpose(T.yt[:, o + b:o + 512:4], T.x[:, o + 128 * b:o + 128 * b + 128]).then_inc(S["tr%d" % i], 1)
+        elif s == "V":
+            v.wait_ge(S["tr%d" % i], 4)
+            for q, d in blocks(k, "v")[lo:hi]:
+                v.tensor_scalar(place(k, q, d), T.yt[32 * q:32 * q + 32, o + 128 * d:o + 128 * d + 128], T.e20[32 * q:32 * q + 32, 0:1],
+                                None, AluOpType.max).then_inc(S["zm%d" % i if q < groups(k) else "cp%d" % i], 1)
+        elif s == "C":
+            gz = groups(k)
+            if gz:
+                v.wait_ge(S["zm%d" % i], made(k)[0])
+                v.tensor_scalar(T["p%d" % i][:, 0:128 * gz], T.z[:, o:o + 128 * gz], T.e20[:, 0:1], None, AluOpType.max).then_inc(S["cp%d" % i], 1)
+        elif s == "Q":
+            v.wait_ge(S["cp%d" % i], made(k)[1])
+            v.quantize_mx(part("pc", i), part("pp", i), T["p%d" % i][:]).then_inc(S["pq%d" % i], 1)
+
+    def scalar(s, k, lo, hi):
+        i = order[k]
+        o = 512 * i
+        if s == "H":
+            a.wait_ge(S["ps%d" % i], 1)
+            a.activation(T.hs[:, 256 * i:256 * i + 256], bank(i, 256, 512), AF.Copy).then_inc(S["hc%d" % i], 1)
+        elif s == "X":
+            a.wait_ge(S["nb%d" % i], 1)
+            a.activation(T.x[:, o:o + 256], bank(i, 0, 256), AF.Exp, bias=shift(i), scale=F).then_inc(S["xa%d" % i], 1)
+            a.activation(T.x[:, o + 256:o + 512], bank(i, 256, 512), AF.Exp, bias=shift(i), scale=F).then_inc(S["xb%d" % i], 1)
+        elif s == "A":
             a.wait_ge(S["tr%d" % i], 4)
-        for q in range(NS):
-            for d in range(4):
-                o = 512 * i + 128 * d
-                a.activation(T["p%d" % i][32 * d:32 * d + 32, 128 * q:128 * q + 128], T.yt[32 * q:32 * q + 32, o:o + 128], AF.Copy).then_inc(S["sc%d" % i], 1)
-        if k + 1 < N:
-            exps(order[k + 1])
-        if k + 2 < N:
-            half(order[k + 2])
-        a.wait_ge(S["pa%d" % i], 1)
-        a.activation(rowbuf(i, 0, 129), bank(i, 0, 129), AF.Copy).then_inc(S["ev%d" % i], 1)
+            for q, d in blocks(k, "a")[lo:hi]:
+                a.activation(place(k, q, d), T.yt[32 * q:32 * q + 32, o + 128 * d:o + 128 * d + 128], AF.Copy).then_inc(S["zm%d" % i], 1)
+        elif s == "E":
+            a.wait_ge(S["pa%d" % i], 1)
+            a.activation(rowbuf(i, 0, 129), bank(i, 0, 129), AF.Copy).then_inc(S["ev%d" % i], 1)
+            if i == rank:
+                a.activation(rowbuf(i, 129, 130), shift(i), AF.Copy).then_inc(S.oc, 1)
+
+    def steps(f, text):
+        for w in text.split():
+            w = w.split(":")
+            f(w[0][0], int(w[0][1:]), int(w[1]) if len(w) > 1 else 0, int(w[2]) if len(w) > 2 else 16)
+
+    steps(scalar, "H0")
+    steps(vector, "M0 N0")
+    v.wait_ge(S.e2, 1)
+    steps(vector, VT)
+    steps(scalar, AT)
 
     for i in order:
         if i == rank:
             continue
-        g.wait_ge(S["ev%d" % i], 2)
+        g.wait_ge(S["ev%d" % i], 1)
         k = W * slot(i, rank)
         if i in relay[rank]:
             loc += send_row(g, T, topo, core, relay[rank][i], rowbuf(i, 0, 130), rowbuf(i, 0, 130), "aa%d" % i)
@@ -295,11 +329,11 @@ def rank_program(g, core, T, topo):
 
     v.wait_ge(S.zc, 2)
     v.wait_ge(S["nb%d" % order[-1]], 1)
-    v.tensor_scalar(T.cc[:, 0:N], T.nb[:, 0:N], -1.0, None, AluOpType.mult).then_inc(S.cn, 1)
+    v.tensor_scalar(T.cc[:, 0:N], T.sb[:, 129:129 + W * (N - 1) + 1:W], -1.0, None, AluOpType.mult).then_inc(S.cn, 1)
     v.wait_ge(S.cn, 1)
     v.transpose(T.ct[:], T.cc[:]).then_inc(S.cx, 1)
-    for i in order:
-        y.wait_ge(S["cp%d" % i], 16)
+    for k, i in enumerate(order):
+        y.wait_ge(S["cp%d" % i], made(k)[1])
         y.dma_start(T.p[i], T["p%d" % i][:]).then_inc(S.st, 16)
     y.wait_ge(S.cx, 1)
     for q in range(4):
@@ -307,7 +341,8 @@ def rank_program(g, core, T, topo):
 
     def arrived(queue, j):
         if j == rank:
-            queue.wait_ge(S["ev%d" % rank], 2)
+            queue.wait_ge(S["ev%d" % rank], 1)
+            queue.wait_ge(S.oc, 1)
         else:
             h = relay[j].get(rank, T.cores[j])
             queue.wait_ge(S["aa%d" % j], bits(topo.mask(h, core)))
@@ -316,76 +351,80 @@ def rank_program(g, core, T, topo):
         lo = W * first + c
         return T.land[:, lo:lo + (n - 1) * W + 1:W]
 
-    E = 6 * W
+    def row(k):
+        return T.land[:, W * k:W * k + 128]
+
+    def term(buf, k, n):
+        return T[buf][:, k:n * 128:n]
+
+    low = T.land[:, ne * W + 129:ne * W + 130]
     for j in early:
         arrived(v, j)
-    v.tensor_reduce(T.sm[:, 0:1], cols(0, 4, 129), AxisListType.X, AluOpType.max, negate=True).then_inc(S.h0, 1)
-    v.wait_ge(S.h0, 1)
-    v.tensor_scalar(T.land[:, E + 129:E + 130], T.sm[:, 0:1], -1.0, None, AluOpType.mult).then_inc(S.h1, 1)
+    v.tensor_reduce(low, cols(0, ne, 129), AxisListType.X, AluOpType.min).then_inc(S.h0, 1)
     a.wait_ge(S.h0, 1)
-    a.activation(T.we[:, 0:4], cols(0, 4, 129), AF.Exp, bias=T.sm[:, 0:1]).then_inc(S.h2, 1)
-    a.wait_ge(S.h2, 1)
-    for k in range(4):
-        a.activation(part("u", k), T.land[:, W * k:W * k + 128], AF.Copy, scale=T.we[:, k:k + 1]).then_inc(S.h3 if k < 2 else S.h4, 1)
-    v.wait_ge(S.h2, 1)
-    v.tensor_tensor(T.pe[:, 0:4], T.we[:, 0:4], cols(0, 4, 128), AluOpType.mult).then_inc(S.h5, 1)
-    v.wait_ge(S.h5, 1)
-    v.tensor_reduce(T.land[:, E + 128:E + 129], T.pe[:, 0:4], AxisListType.X, AluOpType.add).then_inc(S.h6, 1)
-    v.wait_ge(S.h3, 2)
-    v.tensor_tensor(T.v1[:], part("u", 0), part("u", 1), AluOpType.add).then_inc(S.h7, 1)
-    v.wait_ge(S.h4, 2)
-    v.tensor_tensor(T.v2[:], part("u", 2), part("u", 3), AluOpType.add).then_inc(S.h7, 1)
-    v.wait_ge(S.h7, 2)
-    v.tensor_tensor(T.land[:, E:E + 128], T.v1[:], T.v2[:], AluOpType.add).then_inc(S.h8, 1)
-
+    a.activation(T.we[:, 0:ne], cols(0, ne, 129), AF.Exp, bias=low, scale=-1.0).then_inc(S.h1, 1)
+    a.wait_ge(S.h1, 1)
+    for k in range(ne // 2):
+        a.activation(term("ue", k, ne), row(k), AF.Copy, scale=T.we[:, k:k + 1]).then_inc(S.h2, 1)
     v.wait_ge(S.h1, 1)
-    v.wait_ge(S.h6, 1)
-    v.wait_ge(S.h8, 1)
+    v.tensor_tensor(T.pe[:, 0:ne], T.we[:, 0:ne], cols(0, ne, 128), AluOpType.mult).then_inc(S.h3, 1)
+    for k in range(ne // 2, ne):
+        v.tensor_scalar(term("ue", k, ne), row(k), T.we[:, k:k + 1], None, AluOpType.mult).then_inc(S.h4, 1)
+    v.wait_ge(S.h3, 1)
+    v.tensor_reduce(T.land[:, ne * W + 128:ne * W + 129], T.pe[:, 0:ne], AxisListType.X, AluOpType.add).then_inc(S.h5, 1)
+    v.wait_ge(S.f1, 2)
+    v.wait_ge(S.h2, ne // 2)
+    v.wait_ge(S.h4, ne - ne // 2)
+    v.tensor_tensor_scan(T.se[:, 0:ne * 128], T.fe[:, 0:ne * 128], T.ue[:, 0:ne * 128], 0.0, AluOpType.mult, AluOpType.add).then_inc(S.h6, 1)
+
+    v.wait_ge(S.h0, 1)
+    v.wait_ge(S.h5, 1)
     for j in late:
         arrived(v, j)
-    v.tensor_reduce(T.sm[:, 1:2], cols(4, 3, 129), AxisListType.X, AluOpType.max, negate=True).then_inc(S.h9, 1)
-    a.wait_ge(S.h9, 1)
-    a.activation(T.ex[:, 0:3], cols(4, 3, 129), AF.Exp, bias=T.sm[:, 1:2]).then_inc(S.h10, 1)
-    a.wait_ge(S.h10, 1)
-    for k in (4, 5):
-        a.activation(part("u", k), T.land[:, W * k:W * k + 128], AF.Copy, scale=T.ex[:, k - 4:k - 3]).then_inc(S["h%d" % (k + 7)], 1)
+    v.tensor_reduce(T.sm[:, 1:2], cols(ne, nl, 129), AxisListType.X, AluOpType.min).then_inc(S.h7, 1)
+    a.wait_ge(S.h7, 1)
+    a.activation(T.ex[:, 0:nl], cols(ne, nl, 129), AF.Exp, bias=T.sm[:, 1:2], scale=-1.0).then_inc(S.h8, 1)
+    a.wait_ge(S.h8, 1)
+    for k in (nl - 2, nl - 1):
+        a.activation(term("ul", k, nl), row(ne + k), AF.Copy, scale=T.ex[:, k:k + 1]).then_inc(S.h9, 1)
+    v.wait_ge(S.h8, 1)
+    v.tensor_tensor(T.pl[:, 0:nl], T.ex[:, 0:nl], cols(ne, nl, 128), AluOpType.mult).then_inc(S.h10, 1)
+    v.wait_ge(S.h6, 1)
+    v.tensor_scalar(term("ul", 0, nl), term("se", ne - 1, ne), T.ex[:, 0:1], None, AluOpType.mult).then_inc(S.h11, 1)
+    for k in range(1, nl - 2):
+        v.tensor_scalar(term("ul", k, nl), row(ne + k), T.ex[:, k:k + 1], None, AluOpType.mult).then_inc(S.h11, 1)
     v.wait_ge(S.h10, 1)
-    v.tensor_tensor(T.pl[:, 0:3], T.ex[:, 0:3], cols(4, 3, 128), AluOpType.mult).then_inc(S.h13, 1)
-    v.tensor_scalar(part("u", 6), T.land[:, E:E + 128], T.ex[:, 2:3], None, AluOpType.mult).then_inc(S.h16, 1)
-    v.wait_ge(S.h13, 1)
-    v.tensor_reduce(T.sm[:, 2:3], T.pl[:, 0:3], AxisListType.X, AluOpType.add).then_inc(S.h14, 1)
-    v.wait_ge(S.h11, 1)
-    v.wait_ge(S.h16, 1)
-    v.tensor_tensor(T.t1[:], part("u", 4), part("u", 6), AluOpType.add).then_inc(S.h17, 1)
-    v.wait_ge(S.h14, 1)
-    v.reciprocal(T.sm[:, 3:4], T.sm[:, 2:3]).then_inc(S.h15, 1)
-    v.wait_ge(S.h17, 1)
+    v.tensor_reduce(T.sm[:, 2:3], T.pl[:, 0:nl], AxisListType.X, AluOpType.add).then_inc(S.h12, 1)
+    v.wait_ge(S.f2, 2)
+    v.wait_ge(S.h11, nl - 2)
+    v.wait_ge(S.h9, 2)
+    v.tensor_tensor_scan(T.sl[:, 0:nl * 128], T.fl[:, 0:nl * 128], T.ul[:, 0:nl * 128], 0.0, AluOpType.mult, AluOpType.add).then_inc(S.h13, 1)
     v.wait_ge(S.h12, 1)
-    v.tensor_tensor(T.t2[:], T.t1[:], part("u", 5), AluOpType.add).then_inc(S.h18, 1)
-    v.wait_ge(S.h18, 1)
-    v.wait_ge(S.h15, 1)
-    v.tensor_scalar(T.t3[:], T.t2[:], T.sm[:, 3:4], None, AluOpType.mult).then_inc(S.h20, 1)
+    v.reciprocal(T.sm[:, 3:4], T.sm[:, 2:3]).then_inc(S.h14, 1)
     a.wait_ge(S.zc, 2)
     for k, j in enumerate(early):
-        a.activation(T.cw[:, j:j + 1], T.we[:, k:k + 1], AF.Copy, scale=T.ex[:, 2:3]).then_inc(S.h21, 1)
+        a.activation(T.cw[:, j:j + 1], T.we[:, k:k + 1], AF.Copy, scale=T.ex[:, 0:1]).then_inc(S.wx, 1)
     for k, j in enumerate(late):
-        a.activation(T.cw[:, j:j + 1], T.ex[:, k:k + 1], AF.Copy).then_inc(S.h21, 1)
-    v.wait_ge(S.h20, 1)
+        a.activation(T.cw[:, j:j + 1], T.ex[:, k + 1:k + 2], AF.Copy).then_inc(S.wx, 1)
+    v.wait_ge(S.wx, N)
+    v.transpose(T.wt[:], T.cw[:]).then_inc(S.h15, 1)
+    v.wait_ge(S.h13, 1)
+    v.wait_ge(S.h14, 1)
+    v.tensor_scalar(T.t3[:], term("sl", nl - 1, nl), T.sm[:, 3:4], None, AluOpType.mult).then_inc(S.h16, 1)
+    v.wait_ge(S.h16, 1)
     for b in range(4):
-        v.transpose(T.ot[:, 32 * b:32 * b + 32], T.t3[:, b:128:4]).then_inc(S.h19, 1)
-    v.wait_ge(S.h21, N)
-    v.transpose(T.wt[:], T.cw[:]).then_inc(S.cn, 1)
+        v.transpose(T.ot[:, 32 * b:32 * b + 32], T.t3[:, b:128:4]).then_inc(S.cn, 1)
 
-    y.wait_ge(S.h19, 4)
-    a.wait_ge(S.h19, 4)
-    for q in range(4):
-        queue, sem = (y, S.st) if q < 2 else (a, S.st2)
-        queue.dma_start(T.o[:, 32 * q:32 * q + 32], T.ot[32 * q:32 * q + 32, :]).then_inc(sem, 16)
-    y.wait_ge(S.cn, 2)
-    a.wait_ge(S.cn, 2)
+    y.wait_ge(S.h15, 1)
+    a.wait_ge(S.h15, 1)
     for q in range(4):
         queue, sem = (y, S.st) if q < 2 else (a, S.st2)
         queue.dma_start(T.w[:, 32 * q:32 * q + 32], T.wt[32 * q:32 * q + N, 0:32]).then_inc(sem, 16)
+    y.wait_ge(S.cn, 5)
+    a.wait_ge(S.cn, 5)
+    for q in range(4):
+        queue, sem = (y, S.st) if q < 2 else (a, S.st2)
+        queue.dma_start(T.o[:, 32 * q:32 * q + 32], T.ot[32 * q:32 * q + 32, :]).then_inc(sem, 16)
     y.wait_ge(S.st, 16 * (N + 4 + 4))
     a.wait_ge(S.st2, 16 * 4)
     g.wait_ge(S.loc, loc)

import math
from concourse.bass import DstId, RemoteDMATransfer
from concourse.mybir import dt, AluOpType, AxisListType, ActivationFunctionType as AF

N = 6
SIM = 96
W = 132
F = 0.0125
GG = 1

ORDER = [[0, 3, 5, 1, 2, 4], [1, 4, 0, 5, 2, 3], [2, 4, 3, 1, 0, 5], [3, 1, 0, 2, 5, 4], [4, 0, 1, 3, 5, 2], [5, 3, 4, 2, 0, 1]]
QORD = [[4, 3, 1], [3, 4, 0], [5], [5, 0, 2, 4, 1], [2, 5, 1, 0, 3], [0, 4, 1, 2, 3]]
LATE = [[1, 2], [5, 0], [1, 4, 0], [5, 1], [3, 0], [2, 3]]
MOVE = ["aaaavvvvvvvvvvvv"] * 6
VT = ("R0 V0 C0 Q0 M1 N1 R1 M2 V1:0:2 N2 V1:2:16 C1 R2 Q1 M3 V2:0:2 N3 V2:2:16 C2 R3 Q2 M4 V3:0:2 N4 V3:2:16 C3 R4 Q3 "
      "M5 V4:0:2 N5 V4:2:16 C4 R5 Q4 V5 C5 Q5")
AT = "X0 A0 H1 X1 H2 A1 E0 X2 H3 A2 E1 X3 H4 A3 E2 X4 H5 A4 E3 X5 A5 E4 E5"

SCRATCH = {
    "qt": ("sbuf", [128, 512], "bfloat16"),
    "onet": ("sbuf", [128, 512], "bfloat16"),
    "kcd": ("sbuf", [128, 512], "float8_e4m3fn_x4"),
    "ksc": ("sbuf", [128, 512], "uint8"),
    "vo": ("sbuf", [128, 256], "float8_e4m3fn_x4"),
    "vos": ("sbuf", [128, 256], "uint8"),
    "pc": ("sbuf", [128, 128 * N], "float8_e4m3fn_x4"),
    "pp": ("sbuf", [128, 128 * N], "uint8"),
    "hs": ("sbuf", [128, 256 * N], "float32"),
    "mx": ("sbuf", [128, 256 * N], "float32"),
    "x": ("sbuf", [128, 512 * N], "bfloat16"),
    "yt": ("sbuf", [128, 512 * N], "bfloat16"),
    "z": ("sbuf", [128, 512 * N], "bfloat16"),
    "sb": ("sbuf", [128, W * N], "float32"),
    "land": ("sbuf", [128, 7 * W], "float32"),
    "ue": ("sbuf", [128, 512], "float32"),
    "ul": ("sbuf", [128, 512], "float32"),
    "fe": ("sbuf", [128, 512], "float32"),
    "fl": ("sbuf", [128, 512], "float32"),
    "se": ("sbuf", [128, 512], "float32"),
    "sl": ("sbuf", [128, 512], "float32"),
    "m20": ("sbuf", [128, 1], "float32"),
    "e20": ("sbuf", [128, 1], "float32"),
    "cc": ("sbuf", [128, 32], "float32"),
    "ct": ("sbuf", [128, 32], "float32"),
    "cw": ("sbuf", [128, 32], "float32"),
    "wt": ("sbuf", [128, 32], "float32"),
    "we": ("sbuf", [128, 4], "float32"),
    "ex": ("sbuf", [128, 4], "float32"),
    "pe": ("sbuf", [128, 4], "float32"),
    "pl": ("sbuf", [128, 4], "float32"),
    "sm": ("sbuf", [128, 8], "float32"),
    "t3": ("sbuf", [128, 128], "float32"),
    "ot": ("sbuf", [128, 128], "float32"),
    "ps": ("psum", [128, 512 * N], "float32"),
}
for _i in range(N):
    SCRATCH["qc%d" % _i] = ("sbuf", [128, 128], "float8_e4m3fn_x4")
    SCRATCH["qs%d" % _i] = ("sbuf", [128, 128], "uint8")
    SCRATCH["p%d" % _i] = ("sbuf", [128, 512], "bfloat16")

SEMAPHORES = ["lq", "lk", "lv", "loc", "ms", "m2", "e2", "oq", "qq", "st", "st2", "zc", "cn", "cx", "oc", "wx", "f1", "f2"]
for _i in range(N):
    SEMAPHORES += ["%s%d" % (_n, _i) for _n in ("qa", "qb", "aa", "ps", "mx", "nb", "xa", "xb", "hc", "zm", "tr", "cp", "pq", "pa", "ev")]
SEMAPHORES += ["h%d" % _i for _i in range(17)]


def bits(m):
    return bin(m).count("1")


def plan(T, topo):
    relay = []
    for s in range(N):
        src = T.cores[s]
        far = [d for d in range(N) if d != s and not topo.may_write(src, T.cores[d])]
        far.sort(key=lambda d: (topo.chip(T.cores[d]), d))
        r = {}
        if far:
            hs = [h for h in range(SIM) if topo.chip(h) == topo.chip(src) and h not in T.cores
                  and topo.may_write(src, h) and all(topo.may_write(h, T.cores[d]) for d in far)]
            hs.sort(key=lambda h: (topo.die(h) == topo.die(src), h))
            half = (len(far) + 1) // 2
            for k, d in enumerate(far):
                r[d] = hs[0 if k < half else 1]
        relay.append(r)
    return relay


def transfer(T, topo, core, dsts, mask, sem, buf):
    ids = []
    for d in dsts:
        a = topo.addr(d)
        ids.append(DstId(rid=a[0], pnc=a[1]))
    return RemoteDMATransfer(dst_ids=ids, dma_engine_mask=mask, remote_sem=T.sem[sem], srcs=[buf], dsts=[buf for d in dsts])


def slot(home, src):
    late = LATE[home]
    early = [j for j in range(N) if j not in late]
    return len(early) + 1 + late.index(src) if src in late else early.index(src)


def q_parts(T, topo, relay, s):
    src = T.cores[s]
    dst = []
    for h in relay[s].values():
        if h not in dst:
            dst.append(h)
    dst += [T.cores[d] for d in QORD[s]]
    on = [c for c in dst if topo.chip(c) == topo.chip(src)]
    off = [c for c in dst if topo.chip(c) != topo.chip(src)]
    parts = []
    if off:
        m = topo.mask(src, off[0])
        parts.append((off, m))
        parts.append((on, topo.mask(src, on[0]) & ~m))
    else:
        parts.append((on, topo.mask(src, on[0])))
    return parts


def q_count(T, topo, relay, s, dst):
    for cores, m in q_parts(T, topo, relay, s):
        if dst in cores:
            return bits(m)
    h = relay[s][T.rank_of(dst)]
    return bits(topo.mask(h, dst))


def send_row(g, T, topo, core, dst, out, src, sem):
    a = topo.addr(dst)
    m = topo.mask(core, dst)
    g.remote_dma(out_ap=out, in_ap=src, remote_sem=T.sem[sem], local_sem=T.sem["loc"], pid=a[1], routing_id=a[0], dma_engine_mask=m)
    return bits(m)


def helper_program(g, core, T, topo, relay):
    for s in range(N):
        mine = [d for d in relay[s] if relay[s][d] == core]
        if not mine:
            continue
        n = q_count(T, topo, relay, s, core)
        dst = [T.cores[d] for d in mine]
        m = topo.mask(core, dst[0])
        g.wait_ge(T.sem["qa%d" % s], n)
        g.remote_dma_fused([transfer(T, topo, core, dst, m, "qa%d" % s, T["qc%d" % s][:].bitcast(dt.uint8))], local_sem=T.sem["loc"])
        g.wait_ge(T.sem["qb%d" % s], n)
        g.remote_dma_fused([transfer(T, topo, core, dst, m, "qb%d" % s, T["qs%d" % s][:])], local_sem=T.sem["loc"])
        loc = 2 * bits(m)
        for i in ORDER[s]:
            if i in mine:
                g.wait_ge(T.sem["aa%d" % i], bits(topo.mask(T.cores[s], core)))
                k = W * slot(i, s)
                loc += send_row(g, T, topo, core, T.cores[i], T.land[:, k:k + 130], T.sb[:, W * i:W * i + 130], "aa%d" % s)
        g.wait_ge(T.sem["loc"], loc)


def blocks(k, who):
    return [(n // 4, n % 4) for n in range(16) if MOVE[k][n] == who]


def groups(k):
    n = 0
    while n < 4 and MOVE[k][4 * n:4 * n + 4] != "vvvv":
        n += 1
    return n


def rank_program(g, core, T, topo):
    rank = T.rank_of(core)
    relay = plan(T, topo)
    if rank is None:
        helper_program(g, core, T, topo, relay)
        return
    S = T.sem
    v, a, t, y = g.vector, g.scalar, g.tensor, g.sync
    order = ORDER[rank]
    late = LATE[rank]
    early = [j for j in range(N) if j not in late]
    ne, nl = len(early), 1 + len(late)

    def bank(i, lo, hi):
        return T.ps[:, 512 * i + lo:512 * i + hi]

    def rowbuf(i, lo, hi):
        if i == rank:
            k = W * slot(rank, rank)
            return T.land[:, k + lo:k + hi]
        return T.sb[:, W * i + lo:W * i + hi]

    def shift(i):
        return T.sb[:, W * i + 129:W * i + 130]

    def part(buf, i):
        return T[buf][:, 128 * i:128 * i + 128]

    y.dma_start(T.qt[:], T.q[:]).then_inc(S.lq, 16)
    y.dma_start(T.kcd[:].bitcast(dt.uint8), T.kc[:]).then_inc(S.lk, 16)
    y.dma_start(T.ksc[:], T.ks[:]).then_inc(S.lk, 16)
    y.dma_start(T.vo[:, 0:128].bitcast(dt.uint8), T.vc[:]).then_inc(S.lv, 16)
    y.dma_start(T.vos[:, 0:128], T.vs[:]).then_inc(S.lv, 16)

    v.memset(T.m20[:], -20.0).then_inc(S.m2, 1)
    v.memset(T.onet[:], 1.0).then_inc(S.ms, 1)
    v.memset(T.cc[:], 0.0).then_inc(S.zc, 1)
    v.memset(T.cw[:], 0.0).then_inc(S.zc, 1)
    v.wait_ge(S.ms, 1)
    v.quantize_mx(T.vo[:, 128:256], T.vos[:, 128:256], T.onet[:]).then_inc(S.oq, 1)
    v.wait_ge(S.lq, 16)
    v.quantize_mx(T["qc%d" % rank][:], T["qs%d" % rank][:], T.qt[:]).then_inc(S.qq, 1)
    for buf, sem, n in (("fe", S.f1, ne), ("fl", S.f2, nl)):
        v.memset(T[buf][:, 0:n * 128], 1.0).then_inc(sem, 1)
        v.wait_ge(sem, 1)
        v.memset(T[buf][:, 0:n * 128:n], 0.0).then_inc(sem, 1)
    a.wait_ge(S.m2, 1)
    a.activation(T.e20[:], T.m20[:], AF.Exp).then_inc(S.e2, 1)

    loc = 0
    parts = q_parts(T, topo, relay, rank)
    g.wait_ge(S.qq, 1)
    for lo in range(0, max(len(d) for d, m in parts), GG):
        now = [(d[lo:lo + GG], m) for d, m in parts if d[lo:lo + GG]]
        for sem, buf in (("qa%d" % rank, T["qc%d" % rank][:].bitcast(dt.uint8)), ("qb%d" % rank, T["qs%d" % rank][:])):
            g.remote_dma_fused([transfer(T, topo, core, d, m, sem, buf) for d, m in now], local_sem=S.loc)
            loc += sum(bits(m) for d, m in now)

    def scores(i):
        if i == rank:
            t.wait_ge(S.qq, 1)
            t.wait_ge(S.lk, 32)
        else:
            n = q_count(T, topo, relay, i, core)
            t.wait_ge(S["qa%d" % i], n)
            t.wait_ge(S["qb%d" % i], n)
        t.matmul_mx(bank(i, 0, 512), T["qc%d" % i][:], T["qs%d" % i][:], T.kcd[:], T.ksc[:], True, True).then_inc(S["ps%d" % i], 1)

    scores(order[0])
    scores(order[1])
    t.wait_ge(S.lv, 32)
    t.wait_ge(S.oq, 1)
    for k in range(N):
        if k + 2 < N:
            scores(order[k + 2])
        i = order[k]
        t.wait_ge(S["pq%d" % i], 1)
        t.matmul_mx(bank(i, 0, 256), part("pc", i), part("pp", i), T.vo[:, 0:256], T.vos[:, 0:256], True, True).then_inc(S["pa%d" % i], 1)

    def place(k, q, d):
        i = order[k]
        if q < groups(k):
            return T.z[32 * d:32 * d + 32, 512 * i + 128 * q:512 * i + 128 * q + 128]
        return T["p%d" % i][32 * d:32 * d + 32, 128 * q:128 * q + 128]

    def made(k):
        gz = groups(k)
        direct = len([1 for q, d in blocks(k, "v") if q >= gz])
        return 4 * gz, direct + (1 if gz else 0)

    def vector(s, k, lo, hi):
        i = order[k]
        o, m = 512 * i, 256 * i
        if s == "M":
            v.wait_ge(S["hc%d" % i], 1)
            v.tensor_tensor_scan(T.mx[:, m:m + 256], bank(i, 0, 256), T.hs[:, m:m + 256], -1e29, AluOpType.max, AluOpType.max).then_inc(S["mx%d" % i], 1)
        elif s == "N":
            v.wait_ge(S["mx%d" % i], 1)
            v.tensor_scalar(shift(i), T.mx[:, m + 255:m + 256], -F, None, AluOpType.mult).then_inc(S["nb%d" % i], 1)
        elif s == "R":
            for b in range(4):
                if b == 0:
                    v.wait_ge(S["xa%d" % i], 1)
                if b == 2:
                    v.wait_ge(S["xb%d" % i], 1)
                v.transpose(T.yt[:, o + b:o + 512:4], T.x[:, o + 128 * b:o + 128 * b + 128]).then_inc(S["tr%d" % i], 1)
        elif s == "V":
            v.wait_ge(S["tr%d" % i], 4)
            for q, d in blocks(k, "v")[lo:hi]:
                v.tensor_scalar(place(k, q, d), T.yt[32 * q:32 * q + 32, o + 128 * d:o + 128 * d + 128], T.e20[32 * q:32 * q + 32, 0:1],
                                None, AluOpType.max).then_inc(S["zm%d" % i if q < groups(k) else "cp%d" % i], 1)
        elif s == "C":
            gz = groups(k)
            if gz:
                v.wait_ge(S["zm%d" % i], made(k)[0])
                v.tensor_scalar(T["p%d" % i][:, 0:128 * gz], T.z[:, o:o + 128 * gz], T.e20[:, 0:1], None, AluOpType.max).then_inc(S["cp%d" % i], 1)
        elif s == "Q":
            v.wait_ge(S["cp%d" % i], made(k)[1])
            v.quantize_mx(part("pc", i), part("pp", i), T["p%d" % i][:]).then_inc(S["pq%d" % i], 1)

    def scalar(s, k, lo, hi):
        i = order[k]
        o = 512 * i
        if s == "H":
            a.wait_ge(S["ps%d" % i], 1)
            a.activation(T.hs[:, 256 * i:256 * i + 256], bank(i, 256, 512), AF.Copy).then_inc(S["hc%d" % i], 1)
        elif s == "X":
            a.wait_ge(S["nb%d" % i], 1)
            a.activation(T.x[:, o:o + 256], bank(i, 0, 256), AF.Exp, bias=shift(i), scale=F).then_inc(S["xa%d" % i], 1)
            a.activation(T.x[:, o + 256:o + 512], bank(i, 256, 512), AF.Exp, bias=shift(i), scale=F).then_inc(S["xb%d" % i], 1)
        elif s == "A":
            a.wait_ge(S["tr%d" % i], 4)
            for q, d in blocks(k, "a")[lo:hi]:
                a.activation(place(k, q, d), T.yt[32 * q:32 * q + 32, o + 128 * d:o + 128 * d + 128], AF.Copy).then_inc(S["zm%d" % i], 1)
        elif s == "E":
            a.wait_ge(S["pa%d" % i], 1)
            a.activation(rowbuf(i, 0, 129), bank(i, 0, 129), AF.Copy).then_inc(S["ev%d" % i], 1)
            if i == rank:
                a.activation(rowbuf(i, 129, 130), shift(i), AF.Copy).then_inc(S.oc, 1)

    def steps(f, text):
        for w in text.split():
            w = w.split(":")
            f(w[0][0], int(w[0][1:]), int(w[1]) if len(w) > 1 else 0, int(w[2]) if len(w) > 2 else 16)

    steps(scalar, "H0")
    steps(vector, "M0 N0")
    v.wait_ge(S.e2, 1)
    steps(vector, VT)
    steps(scalar, AT)

    for i in order:
        if i == rank:
            continue
        g.wait_ge(S["ev%d" % i], 1)
        k = W * slot(i, rank)
        if i in relay[rank]:
            loc += send_row(g, T, topo, core, relay[rank][i], rowbuf(i, 0, 130), rowbuf(i, 0, 130), "aa%d" % i)
        else:
            loc += send_row(g, T, topo, core, T.cores[i], T.land[:, k:k + 130], rowbuf(i, 0, 130), "aa%d" % rank)

    v.wait_ge(S.zc, 2)
    v.wait_ge(S["nb%d" % order[-1]], 1)
    v.tensor_scalar(T.cc[:, 0:N], T.sb[:, 129:129 + W * (N - 1) + 1:W], -1.0, None, AluOpType.mult).then_inc(S.cn, 1)
    v.wait_ge(S.cn, 1)
    v.transpose(T.ct[:], T.cc[:]).then_inc(S.cx, 1)
    for k, i in enumerate(order):
        y.wait_ge(S["cp%d" % i], made(k)[1])
        y.dma_start(T.p[i], T["p%d" % i][:]).then_inc(S.st, 16)
    y.wait_ge(S.cx, 1)
    for q in range(4):
        y.dma_start(T.c[:, 32 * q:32 * q + 32], T.ct[32 * q:32 * q + N, 0:32]).then_inc(S.st, 16)

    def arrived(queue, j):
        if j == rank:
            queue.wait_ge(S["ev%d" % rank], 1)
            queue.wait_ge(S.oc, 1)
        else:
            h = relay[j].get(rank, T.cores[j])
            queue.wait_ge(S["aa%d" % j], bits(topo.mask(h, core)))

    def cols(first, n, c):
        lo = W * first + c
        return T.land[:, lo:lo + (n - 1) * W + 1:W]

    def row(k):
        return T.land[:, W * k:W * k + 128]

    def term(buf, k, n):
        return T[buf][:, k:n * 128:n]

    low = T.land[:, ne * W + 129:ne * W + 130]
    for j in early:
        arrived(v, j)
    v.tensor_reduce(low, cols(0, ne, 129), AxisListType.X, AluOpType.min).then_inc(S.h0, 1)
    a.wait_ge(S.h0, 1)
    a.activation(T.we[:, 0:ne], cols(0, ne, 129), AF.Exp, bias=low, scale=-1.0).then_inc(S.h1, 1)
    a.wait_ge(S.h1, 1)
    for k in range(ne // 2):
        a.activation(term("ue", k, ne), row(k), AF.Copy, scale=T.we[:, k:k + 1]).then_inc(S.h2, 1)
    v.wait_ge(S.h1, 1)
    v.tensor_tensor(T.pe[:, 0:ne], T.we[:, 0:ne], cols(0, ne, 128), AluOpType.mult).then_inc(S.h3, 1)
    for k in range(ne // 2, ne):
        v.tensor_scalar(term("ue", k, ne), row(k), T.we[:, k:k + 1], None, AluOpType.mult).then_inc(S.h4, 1)
    v.wait_ge(S.h3, 1)
    v.tensor_reduce(T.land[:, ne * W + 128:ne * W + 129], T.pe[:, 0:ne], AxisListType.X, AluOpType.add).then_inc(S.h5, 1)
    v.wait_ge(S.f1, 2)
    v.wait_ge(S.h2, ne // 2)
    v.wait_ge(S.h4, ne - ne // 2)
    v.tensor_tensor_scan(T.se[:, 0:ne * 128], T.fe[:, 0:ne * 128], T.ue[:, 0:ne * 128], 0.0, AluOpType.mult, AluOpType.add).then_inc(S.h6, 1)

    v.wait_ge(S.h0, 1)
    v.wait_ge(S.h5, 1)
    for j in late:
        arrived(v, j)
    v.tensor_reduce(T.sm[:, 1:2], cols(ne, nl, 129), AxisListType.X, AluOpType.min).then_inc(S.h7, 1)
    a.wait_ge(S.h7, 1)
    a.activation(T.ex[:, 0:nl], cols(ne, nl, 129), AF.Exp, bias=T.sm[:, 1:2], scale=-1.0).then_inc(S.h8, 1)
    a.wait_ge(S.h8, 1)
    for k in (nl - 2, nl - 1):
        a.activation(term("ul", k, nl), row(ne + k), AF.Copy, scale=T.ex[:, k:k + 1]).then_inc(S.h9, 1)
    v.wait_ge(S.h8, 1)
    v.tensor_tensor(T.pl[:, 0:nl], T.ex[:, 0:nl], cols(ne, nl, 128), AluOpType.mult).then_inc(S.h10, 1)
    v.wait_ge(S.h6, 1)
    v.tensor_scalar(term("ul", 0, nl), term("se", ne - 1, ne), T.ex[:, 0:1], None, AluOpType.mult).then_inc(S.h11, 1)
    for k in range(1, nl - 2):
        v.tensor_scalar(term("ul", k, nl), row(ne + k), T.ex[:, k:k + 1], None, AluOpType.mult).then_inc(S.h11, 1)
    v.wait_ge(S.h10, 1)
    v.tensor_reduce(T.sm[:, 2:3], T.pl[:, 0:nl], AxisListType.X, AluOpType.add).then_inc(S.h12, 1)
    v.wait_ge(S.f2, 2)
    v.wait_ge(S.h11, nl - 2)
    v.wait_ge(S.h9, 2)
    v.tensor_tensor_scan(T.sl[:, 0:nl * 128], T.fl[:, 0:nl * 128], T.ul[:, 0:nl * 128], 0.0, AluOpType.mult, AluOpType.add).then_inc(S.h13, 1)
    v.wait_ge(S.h12, 1)
    v.reciprocal(T.sm[:, 3:4], T.sm[:, 2:3]).then_inc(S.h14, 1)
    a.wait_ge(S.zc, 2)
    for k, j in enumerate(early):
        a.activation(T.cw[:, j:j + 1], T.we[:, k:k + 1], AF.Copy, scale=T.ex[:, 0:1]).then_inc(S.wx, 1)
    for k, j in enumerate(late):
        a.activation(T.cw[:, j:j + 1], T.ex[:, k + 1:k + 2], AF.Copy).then_inc(S.wx, 1)
    v.wait_ge(S.wx, N)
    v.transpose(T.wt[:], T.cw[:]).then_inc(S.h15, 1)
    v.wait_ge(S.h13, 1)
    v.wait_ge(S.h14, 1)
    v.tensor_scalar(T.t3[:], term("sl", nl - 1, nl), T.sm[:, 3:4], None, AluOpType.mult).then_inc(S.h16, 1)
    v.wait_ge(S.h16, 1)
    for b in range(4):
        v.transpose(T.ot[:, 32 * b:32 * b + 32], T.t3[:, b:128:4]).then_inc(S.cn, 1)

    y.wait_ge(S.h15, 1)
    a.wait_ge(S.h15, 1)
    for q in range(4):
        queue, sem = (y, S.st) if q < 2 else (a, S.st2)
        queue.dma_start(T.w[:, 32 * q:32 * q + 32], T.wt[32 * q:32 * q + N, 0:32]).then_inc(sem, 16)
    y.wait_ge(S.cn, 5)
    a.wait_ge(S.cn, 5)
    for q in range(4):
        queue, sem = (y, S.st) if q < 2 else (a, S.st2)
        queue.dma_start(T.o[:, 32 * q:32 * q + 32], T.ot[32 * q:32 * q + 32, :]).then_inc(sem, 16)
    y.wait_ge(S.st, 16 * (N + 4 + 4))
    a.wait_ge(S.st2, 16 * 4)
    g.wait_ge(S.loc, loc)
